import numpy as np
import ml_dtypes


def mxq(x, axis, fmt="e4m3"):
    dtype, down = {"e4m3": (ml_dtypes.float8_e4m3fn, 7), "e5m2": (ml_dtypes.float8_e5m2, 14)}[fmt]
    v = np.moveaxis(np.asarray(x, np.float32).astype(ml_dtypes.bfloat16).astype(np.float64), axis, -1)
    blocks = v.reshape(v.shape[:-1] + (-1, 32))
    amax = np.abs(blocks).max(-1, keepdims=True)
    byte = np.maximum(np.where(amax > 0, np.frexp(amax)[1] - 1 + 127, 0) - down, 1)
    scale = np.exp2(byte - 127.0)
    codes = (blocks / scale).astype(np.float32).astype(dtype).astype(np.float64)
    return np.moveaxis((codes * scale).reshape(v.shape), -1, axis)


WIDE = False


def mx_kscale(k):
    if not WIDE:
        return np.ones(k)
    levels = np.array([10, -10, 5, -5, 0])
    if k % 512:
        return np.exp2(np.random.permutation(np.resize(levels, k // 32))).repeat(32)
    a = np.empty((k // 512, 16))
    for p in range(k // 512):
        a[p, :8] = np.random.permutation(np.resize(levels, 8))
        for g in range(8):
            far = levels[np.abs(levels - a[p, g]) >= 10]
            a[p, g + 8] = far[np.random.randint(len(far))]
    return np.exp2(a.ravel()).repeat(32)


BF16 = ml_dtypes.bfloat16


def bf(x):
    return np.asarray(x, np.float32).astype(BF16)


def f64(x):
    return np.asarray(x).astype(np.float64)


E2M1 = np.array([0.0, 0.5, 1.0, 1.5, 2.0, 3.0, 4.0, 6.0, -0.0, -0.5, -1.0, -1.5, -2.0, -3.0, -4.0, -6.0])


def pack_weight(w, fmt):
    k, n = w.shape
    w = f64(bf(w)).reshape(k // 32, 32, n)
    amax = np.abs(w).max(1)
    if fmt == "e4m3":
        byte = np.frexp(amax)[1] - 1 + 127 - 7
    else:
        mant, ex = np.frexp(amax / 6.0)
        byte = np.where(mant > 0.5, ex, ex - 1) + 127
    byte = np.clip(np.where(amax > 0, byte, 1), 1, 254)
    scaled = (w * np.exp2(127.0 - byte)[:, None, :]).reshape(k, n).astype(np.float32)
    by_word = np.ascontiguousarray(scaled.reshape(k // 512, 128, 4, n).transpose(0, 1, 3, 2))
    if fmt == "e4m3":
        words = by_word.astype(ml_dtypes.float8_e4m3fn).view(np.uint8)
    else:
        c = by_word.astype(ml_dtypes.float4_e2m1fn).view(np.uint8) & 0xF
        words = c[..., 0::2] | (c[..., 1::2] << 4)
    return np.ascontiguousarray(words), np.ascontiguousarray(byte.astype(np.uint8).reshape(k // 512, 16, n))


def unpack_weight(words, scales, fmt):
    g, p, n, _ = words.shape
    if fmt == "e4m3":
        vals = np.ascontiguousarray(words).view(ml_dtypes.float8_e4m3fn).astype(np.float64)
    else:
        nib = np.empty((g, p, n, 4), np.uint8)
        nib[..., 0::2] = words & 0xF
        nib[..., 1::2] = words >> 4
        vals = E2M1[nib]
    vals = vals * np.repeat(np.exp2(scales.astype(np.float64) - 127.0), 8, axis=1)[..., None]
    return vals.transpose(0, 1, 3, 2).reshape(g * 512, n)
def pack4(w):
    words, scales = pack_weight(w, "e2m1")
    return words.reshape(words.shape[0], 128, -1), scales


def unpack4(words, scales):
    return unpack_weight(words.reshape(words.shape[0], 128, -1, 2), scales, "e2m1")


def planes(Y):
    n, m = Y.shape
    b = f64(bf(Y)).reshape(n // 32, 32, m)
    amax = np.abs(b).max(1)
    byte = np.clip(np.where(amax > 0, np.frexp(amax)[1] - 1 + 127 - 7, 1), 1, 254)
    codes = (b * np.exp2(127.0 - byte)[:, None, :]).reshape(n, m).astype(np.float32).astype(ml_dtypes.float8_e4m3fn).view(np.uint8)
    words = codes.reshape(n // 512, 128, 4, m).transpose(0, 1, 3, 2)
    return np.ascontiguousarray(words), np.ascontiguousarray(byte.astype(np.uint8).reshape(n // 512, 16, m))


M, K, N = 1280, 1536, 2048
HALO = 0.25
SPREAD = 0.8


def speckle_blur():
    scene = (np.arange(K) + 0.5) / K
    detector = (np.arange(N) + 0.5) / N
    offset = (scene[:, None] - detector[None, :]) / HALO
    speckle = 0.5 * (np.random.randn(K, N) ** 2 + np.random.randn(K, N) ** 2)
    return speckle / (1.0 + offset ** 2) / K


def setup_inputs():
    s = mx_kscale(K)
    estimate = np.exp(1.2 * np.random.randn(M, K))
    x_words, x_scales = pack_weight(f64(bf(estimate.T / s[:, None])), "e4m3")
    return {
        "x_words": x_words,
        "x_scales": x_scales,
        "blur": bf(speckle_blur() * s[:, None]),
        "measured": bf(np.exp(0.4 * np.random.randn(M, N))),
        "background": bf(0.4 * np.exp(0.5 * np.random.randn(N))),
        "weight": bf(np.exp(SPREAD * np.random.randn(N))),
    }


def reference(x_words, x_scales, blur, measured, background, weight):
    X_t = unpack_weight(x_words, x_scales, "e4m3")
    Bq = mxq(f64(blur), 0, "e4m3")
    blurred = X_t.T @ Bq
    predicted = blurred + f64(background)
    y = f64(measured) / predicted * f64(weight)
    Y = y.T
    words, scales = planes(Y)
    return y, words, scales

@@ -1,0 +1,335 @@
+from contextlib import ExitStack
+
+import concourse.mybir as mybir
+from concourse.masks import make_identity
+
+M, K, N = 1280, 1536, 2048
+FLOPS = 2 * M * K * N
+
+F32 = mybir.dt.float32
+BF16 = mybir.dt.bfloat16
+I32 = mybir.dt.int32
+U32 = mybir.dt.uint32
+U8 = mybir.dt.uint8
+FP8X4 = mybir.dt.float8_e4m3fn_x4
+ACT = mybir.ActivationFunctionType
+ALU = mybir.AluOpType
+
+P = 128
+PASSES = K // 512
+GROUPS = N // 512
+CHUNKS = ((0, 512), (512, 512), (1024, 256))
+STEPS = [
+    (g, ch, h)
+    for g in range(GROUPS)
+    for ch, h in ((0, 0), (0, 1), (1, 0), (1, 1), (2, None))
+]
+NSTEP = len(STEPS)
+PIECES = [(g, h, c) for g in range(GROUPS) for h in range(2) for c in range(PASSES)]
+
+
+def tile_weighted_lucy_ratio_g6_kernel(
+    tc, x_words, x_scales, blur, measured, background, weight, out_0, out_1, out_2
+):
+    nc = tc.nc
+    with ExitStack() as ctx:
+        keep = ctx.enter_context(tc.tile_pool(name="keep", bufs=1))
+        work = ctx.enter_context(tc.tile_pool(name="work", bufs=3))
+        psum = ctx.enter_context(tc.psum_pool(name="psum", bufs=3))
+        ctx.enter_context(tc.manual_schedule())
+
+        xw = keep.tile([P, PASSES, M], U32, align_bytes=64)
+        xs = keep.tile([P, PASSES, M], U8, align_bytes=64)
+        bcodes = keep.tile([P, PASSES, N], U32, align_bytes=64)
+        bscales = keep.tile([P, PASSES, N], U8, align_bytes=64)
+        ycodes = keep.tile([P, GROUPS, M], U32, align_bytes=64)
+        yscales = keep.tile([P, GROUPS, M], U8, align_bytes=64)
+        ident = keep.tile([P, P], F32)
+        vec_rows = keep.tile([32, P], BF16)
+        vec_wide = keep.tile([P, P], F32)
+        inv_w = keep.tile([P, 16], F32)
+        bias = keep.tile([P, 16], F32)
+        one = keep.tile([P, 1], F32)
+        warm = keep.tile([P, 1], F32)
+
+        raw = {}
+        grouped = {}
+        meas = {}
+        recip = {}
+        turned = {}
+        ytile = {}
+        ypairs = {}
+        pairs_ps = {}
+        yquads = {}
+
+        def load_blur(g, c, h):
+            rows = blur[512 * c : 512 * (c + 1), :].rearrange("(p t) n -> p t n", t=4)
+            if h is None:
+                t = work.tile([P, 4, 512], BF16, name="raw", tag="raw", bufs=6)
+                nc.sync.dma_start(out=t[:], in_=rows[:, :, 512 * g : 512 * (g + 1)])
+                raw[g, 0, c] = t[:, :, 0:256]
+                raw[g, 1, c] = t[:, :, 256:512]
+            else:
+                t = work.tile([P, 4, 256], BF16, name="raw_half", tag="raw_half", bufs=6)
+                n0 = 512 * g + 256 * h
+                nc.sync.dma_start(out=t[:], in_=rows[:, :, n0 : n0 + 256])
+                raw[g, h, c] = t[:]
+
+        def load_x(ch):
+            m0, w = CHUNKS[ch]
+            src = x_words.rearrange("c p m t -> p c (m t)")[:, :, 4 * m0 : 4 * (m0 + w)]
+            nc.sync.dma_start(out=xw[:, :, m0 : m0 + w].bitcast(I32), in_=src.bitcast(I32))
+
+        def load_meas(g, ch):
+            m0, w = CHUNKS[ch]
+            t = work.tile([P, w // P, 512], BF16, name="meas", tag="meas", bufs=6)
+            src = measured[m0 : m0 + w, 512 * g : 512 * (g + 1)]
+            nc.sync.dma_start(out=t[:], in_=src.rearrange("(a p) n -> p a n", p=P))
+            meas[g, ch] = t
+
+        def interleave(i, on_scalar):
+            t = work.tile([P, 256, 4], BF16, name="grouped", tag="grouped", bufs=4, align_bytes=64)
+            dst = t[:].rearrange("p (c i) t -> p c t i", i=4)
+            src = raw[PIECES[i]].rearrange("p t (c i) -> p c t i", i=4)
+            if on_scalar:
+                nc.scalar.copy(out=dst, in_=src)
+            else:
+                nc.vector.tensor_copy(out=dst, in_=src)
+            grouped[i] = t
+
+        def quantize_blur(i):
+            g, h, c = PIECES[i]
+            cols = slice(512 * g + 256 * h, 512 * g + 256 * (h + 1))
+            nc.vector.quantize_mx(
+                out=bcodes[:, c, cols].bitcast(FP8X4),
+                scales=bscales[:, c, cols],
+                in_=grouped[i][:].rearrange("p n t -> p (n t)"),
+            )
+
+        def step_tiles(s, b):
+            g, ch, h = STEPS[s]
+            if h is None:
+                return [4 * g + 2 * b, 4 * g + 2 * b + 1]
+            return [4 * g + 2 * h + b]
+
+        def product(s, b):
+            g, ch, h = STEPS[s]
+            m0, w = CHUNKS[ch]
+            if b == 0:
+                recip[s] = work.tile([P, 1024], F32, name="recip", tag="recip", bufs=3)
+            acc = psum.tile([P, 512], F32, name="acc", tag="acc", bufs=3)
+            for i, j in enumerate(step_tiles(s, b)):
+                for c in range(PASSES):
+                    nc.tensor.matmul_mx(
+                        out=acc[:, w * i : w * (i + 1)],
+                        lhsT=bcodes[:, c, P * j : P * (j + 1)].bitcast(FP8X4),
+                        lhsT_scale=bscales[:, c, P * j : P * (j + 1)],
+                        rhs=xw[:, c, m0 : m0 + w].bitcast(FP8X4),
+                        rhs_scale=xs[:, c, m0 : m0 + w],
+                        start=(c == 0),
+                        stop=(c == PASSES - 1),
+                    )
+            for i, j in enumerate(step_tiles(s, b)):
+                nc.scalar.activation(
+                    out=recip[s][:, 512 * b + w * i : 512 * b + w * (i + 1)],
+                    in_=acc[:, w * i : w * (i + 1)],
+                    func=ACT.Abs_reciprocal_sqrt,
+                    bias=bias[:, j : j + 1],
+                    scale=inv_w[:, j : j + 1],
+                )
+
+        def square(s, b):
+            half = recip[s][:, 512 * b : 512 * (b + 1)]
+            nc.scalar.activation(out=half, in_=half, func=ACT.Square)
+
+        def turn(s, b):
+            g, ch, h = STEPS[s]
+            m0, w = CHUNKS[ch]
+            bank = psum.tile([P, 512], F32, name="turned", tag="turned", bufs=3)
+            q = recip[s][:].rearrange("p (j m) -> p j m", m=w)
+            if h is None:
+                blocks = [(j, b) for j in range(4)]
+            else:
+                blocks = [(j, 2 * b + a) for a in range(2) for j in range(2)]
+            for i, (j, a) in enumerate(blocks):
+                nc.tensor.transpose(bank[:, P * i : P * (i + 1)], q[:, j, P * a : P * (a + 1)], ident[:])
+            turned[s, b] = bank
+
+        def multiply(s, b):
+            g, ch, h = STEPS[s]
+            m0, w = CHUNKS[ch]
+            if b == 0 and h != 1:
+                ytile[g, ch] = work.tile([P, w // P, 512], F32, name="y", tag="y", bufs=6)
+            y = ytile[g, ch]
+            if h is None:
+                nc.vector.tensor_tensor(
+                    out=y[:, b, :], in0=turned[s, b][:], in1=meas[g, ch][:, b, :], op=ALU.mult
+                )
+            else:
+                rows = slice(2 * b, 2 * b + 2)
+                cols = slice(256 * h, 256 * (h + 1))
+                nc.vector.tensor_tensor(
+                    out=y[:, rows, cols],
+                    in0=turned[s, b][:].rearrange("p (a n) -> p a n", a=2),
+                    in1=meas[g, ch][:, rows, cols],
+                    op=ALU.mult,
+                )
+
+        def store_y(s):
+            g, ch, h = STEPS[s]
+            m0, w = CHUNKS[ch]
+            dst = out_0[m0 : m0 + w, 512 * g : 512 * (g + 1)]
+            nc.sync.dma_start(out=dst.rearrange("(a p) n -> p a n", p=P), in_=ytile[g, ch][:])
+
+        def round_y(s):
+            g, ch, h = STEPS[s]
+            m0, w = CHUNKS[ch]
+            if h != 1:
+                ypairs[g, ch] = work.tile([P, w // P, 2, P, 2], BF16, name="ypairs", tag="ypairs", bufs=3)
+            dst = ypairs[g, ch]
+            y = ytile[g, ch]
+            if h is None:
+                nc.vector.tensor_copy(
+                    out=dst[:], in_=y[:].rearrange("m a (p u e) -> m a u p e", u=2, e=2)
+                )
+            else:
+                nc.vector.tensor_copy(
+                    out=dst[:, :, :, 64 * h : 64 * (h + 1), :],
+                    in_=y[:, :, 256 * h : 256 * (h + 1)].rearrange("m a (p u e) -> m a u p e", u=2, e=2),
+                )
+
+        def turn_pairs(k):
+            g, r = divmod(k, 5)
+            words = ypairs[g, r // 2][:].rearrange("m a u p e -> m a u (p e)").bitcast(F32)
+            bank = psum.tile([P, 2, 2, P], F32, name="pairs", tag="pairs", bufs=2)
+            for a in range(2):
+                for u in range(2):
+                    nc.tensor.transpose(bank[:, a, u, :], words[:, 2 * (r % 2) + a, u, :], ident[:])
+            pairs_ps[k] = bank
+
+        def gather_quads(k, on_scalar):
+            t = work.tile([P, 1024], BF16, name="yquads", tag="yquads", bufs=3, align_bytes=64)
+            dst = t[:].bitcast(F32).rearrange("p (a m u) -> p a m u", a=2, u=2)
+            src = pairs_ps[k][:].rearrange("p a u m -> p a m u")
+            if on_scalar:
+                nc.scalar.copy(out=dst, in_=src)
+            else:
+                nc.vector.tensor_copy(out=dst, in_=src)
+            yquads[k] = t
+
+        def quantize_y(k):
+            g, r = divmod(k, 5)
+            cols = slice(256 * r, 256 * (r + 1))
+            nc.vector.quantize_mx(
+                out=ycodes[:, g, cols].bitcast(FP8X4), scales=yscales[:, g, cols], in_=yquads[k][:]
+            )
+
+        def store_codes(g, m0, m1):
+            dst = out_1[g].rearrange("p m t -> p (m t)")[:, 4 * m0 : 4 * m1]
+            nc.sync.dma_start(out=dst.bitcast(I32), in_=ycodes[:, g, m0:m1].bitcast(I32))
+
+        def store_scales(g0, g1):
+            for quad in range(4):
+                dst = out_2[g0:g1, 4 * quad : 4 * quad + 4, :].rearrange("g r m -> r g m")
+                nc.sync.dma_start(
+                    out=dst.bitcast(I32), in_=yscales[32 * quad : 32 * quad + 4, g0:g1, :].bitcast(I32)
+                )
+
+        nc.vector.memset(one[:], 1.0)
+        nc.scalar.activation(out=warm[:], in_=one[:], func=ACT.Abs_reciprocal_sqrt)
+        nc.vector.memset(xs[:].bitcast(I32), 0)
+        make_identity(nc, ident[:])
+        nc.gpsimd.memset(vec_wide[:], 0.0)
+        for c in range(PASSES):
+            load_blur(0, c, 0)
+        for quad in range(4):
+            src = x_scales[:, 4 * quad : 4 * quad + 4, :].rearrange("c r m -> r c m")
+            nc.sync.dma_start(out=xs[32 * quad : 32 * quad + 4, :, :].bitcast(I32), in_=src.bitcast(I32))
+        nc.sync.dma_start(out=vec_rows[0:16, :], in_=background.rearrange("(j p) -> j p", p=P))
+        nc.sync.dma_start(out=vec_rows[16:32, :], in_=weight.rearrange("(j p) -> j p", p=P))
+        load_x(0)
+        for c in range(PASSES):
+            load_blur(0, c, 1)
+        load_meas(0, 0)
+        load_x(1)
+        for c in range(PASSES):
+            load_blur(1, c, None)
+        load_meas(0, 1)
+        load_x(2)
+        load_meas(0, 2)
+        for c in range(PASSES):
+            load_blur(2, c, None)
+        load_meas(1, 0)
+
+        interleave(0, False)
+        interleave(1, True)
+        interleave(2, False)
+        quantize_blur(0)
+        nc.vector.tensor_copy(out=vec_wide[0:32, :], in_=vec_rows[:])
+        quantize_blur(1)
+        vec_ps = psum.tile([P, 2, 2, P], F32, name="pairs", tag="pairs", bufs=2)
+        nc.tensor.transpose(vec_ps[:, 0, 0, :], vec_wide[:], ident[:])
+        quantize_blur(2)
+        nc.vector.reciprocal(out=inv_w[:], in_=vec_ps[:, 0, 0, 16:32])
+        nc.vector.tensor_tensor(out=bias[:], in0=vec_ps[:, 0, 0, 0:16], in1=inv_w[:], op=ALU.mult)
+
+        vector_pieces = {0: [3, 4, 5], 2: [6, 7], 3: [9], 15: [22, 23]}
+        for s in range(4, 15):
+            vector_pieces[s] = [s + 7]
+        scalar_pieces = {2: [8], 3: [10]}
+        meas_loads = {5 * g + 2 * ch + 1 - 4: (g, ch) for g in range(GROUPS) for ch in range(3)}
+
+        pending = []
+        for s in range(NSTEP + 5):
+            if s >= 3 and s in meas_loads:
+                load_meas(*meas_loads[s])
+            if 6 <= s <= 8:
+                load_blur(3, s - 6, None)
+            if s < NSTEP:
+                product(s, 0)
+            mine = vector_pieces.get(s, [])
+            for i in mine[:1]:
+                interleave(i, False)
+            if 0 <= s - 5 < NSTEP and not mine:
+                quantize_y(s - 5)
+            if 0 <= s - 2 < NSTEP:
+                round_y(s - 2)
+            if 0 <= s - 5 < NSTEP and mine:
+                quantize_y(s - 5)
+            for i in pending:
+                quantize_blur(i)
+            pending = []
+            for n, i in enumerate(mine):
+                if n + 1 < len(mine):
+                    interleave(mine[n + 1], False)
+                quantize_blur(i)
+            if s < NSTEP:
+                product(s, 1)
+                square(s, 0)
+            if 0 <= s - 1 < NSTEP:
+                turn(s - 1, 0)
+                turn(s - 1, 1)
+            if 0 <= s - 3 < NSTEP:
+                turn_pairs(s - 3)
+            for i in scalar_pieces.get(s, []):
+                interleave(i, True)
+                pending.append(i)
+            if 0 <= s - 4 < NSTEP:
+                gather_quads(s - 4, s < 17)
+            if s < NSTEP:
+                square(s, 1)
+            if 0 <= s - 1 < NSTEP:
+                multiply(s - 1, 0)
+                multiply(s - 1, 1)
+                if STEPS[s - 1][2] != 0:
+                    store_y(s - 1)
+            k = s - 5
+            if k in (4, 9, 14):
+                store_codes(k // 5, 0, M)
+            if k == 14:
+                store_scales(0, 3)
+            if k == 18:
+                store_codes(3, 0, 1024)
+            if k == 19:
+                store_codes(3, 1024, M)
+                store_scales(3, 4)

@@ -18,14 +18,10 @@ ALU = mybir.AluOpType
 P = 128
 PASSES = K // 512
 GROUPS = N // 512
-CHUNKS = ((0, 512), (512, 512), (1024, 256))
-STEPS = [
-    (g, ch, h)
-    for g in range(GROUPS)
-    for ch, h in ((0, 0), (0, 1), (1, 0), (1, 1), (2, None))
-]
-NSTEP = len(STEPS)
-PIECES = [(g, h, c) for g in range(GROUPS) for h in range(2) for c in range(PASSES)]
+W = 256
+CHUNKS = M // W
+NSTEP = GROUPS * CHUNKS
+PIECES = [(g, c, h) for g in range(GROUPS) for c in range(PASSES) for h in range(2)]
 
 
 def tile_weighted_lucy_ratio_g6_kernel(
@@ -62,43 +58,48 @@ def tile_weighted_lucy_ratio_g6_kernel(
         pairs_ps = {}
         yquads = {}
 
-        def load_blur(g, c, h):
+        def load_blur(g, c, ng):
             rows = blur[512 * c : 512 * (c + 1), :].rearrange("(p t) n -> p t n", t=4)
-            if h is None:
-                t = work.tile([P, 4, 512], BF16, name="raw", tag="raw", bufs=6)
-                nc.sync.dma_start(out=t[:], in_=rows[:, :, 512 * g : 512 * (g + 1)])
-                raw[g, 0, c] = t[:, :, 0:256]
-                raw[g, 1, c] = t[:, :, 256:512]
-            else:
-                t = work.tile([P, 4, 256], BF16, name="raw_half", tag="raw_half", bufs=6)
-                n0 = 512 * g + 256 * h
-                nc.sync.dma_start(out=t[:], in_=rows[:, :, n0 : n0 + 256])
-                raw[g, h, c] = t[:]
+            t = work.tile([P, 4, 512 * ng], BF16, name="raw%d" % ng, tag="raw%d" % ng, bufs=6 // ng)
+            nc.sync.dma_start(out=t[:], in_=rows[:, :, 512 * g : 512 * (g + ng)])
+            for i in range(2 * ng):
+                raw[g + i // 2, c, i % 2] = t[:, :, 256 * i : 256 * (i + 1)]
 
-        def load_x(ch):
-            m0, w = CHUNKS[ch]
-            src = x_words.rearrange("c p m t -> p c (m t)")[:, :, 4 * m0 : 4 * (m0 + w)]
-            nc.sync.dma_start(out=xw[:, :, m0 : m0 + w].bitcast(I32), in_=src.bitcast(I32))
+        def load_x(r0, r1):
+            src = x_words.rearrange("c p m t -> p c (m t)")[:, :, 4 * W * r0 : 4 * W * r1]
+            nc.sync.dma_start(out=xw[:, :, W * r0 : W * r1].bitcast(I32), in_=src.bitcast(I32))
 
-        def load_meas(g, ch):
-            m0, w = CHUNKS[ch]
-            t = work.tile([P, w // P, 512], BF16, name="meas", tag="meas", bufs=6)
-            src = measured[m0 : m0 + w, 512 * g : 512 * (g + 1)]
+        def load_meas(g, r, ng, nr):
+            t = work.tile([P, 2 * nr, 512 * ng], BF16, name="meas", tag="meas", bufs=8)
+            src = measured[W * r : W * (r + nr), 512 * g : 512 * (g + ng)]
             nc.sync.dma_start(out=t[:], in_=src.rearrange("(a p) n -> p a n", p=P))
-            meas[g, ch] = t
+            for i in range(ng):
+                for j in range(nr):
+                    meas[CHUNKS * (g + i) + r + j] = t[:, 2 * j : 2 * j + 2, 512 * i : 512 * (i + 1)]
 
-        def interleave(i, on_scalar):
-            t = work.tile([P, 256, 4], BF16, name="grouped", tag="grouped", bufs=4, align_bytes=64)
-            dst = t[:].rearrange("p (c i) t -> p c t i", i=4)
-            src = raw[PIECES[i]].rearrange("p t (c i) -> p c t i", i=4)
-            if on_scalar:
-                nc.scalar.copy(out=dst, in_=src)
+        def interleave(i, eng):
+            if eng == "g":
+                t = work.tile([P, 256, 4], BF16, name="slow", tag="slow", bufs=1, align_bytes=64)
+                nc.gpsimd.tensor_scalar(
+                    out=t[:],
+                    in0=raw[PIECES[i]].rearrange("p t n -> p n t"),
+                    scalar1=1.0,
+                    scalar2=0.0,
+                    op0=ALU.mult,
+                    op1=ALU.add,
+                )
             else:
-                nc.vector.tensor_copy(out=dst, in_=src)
+                t = work.tile([P, 256, 4], BF16, name="grouped", tag="grouped", bufs=4, align_bytes=64)
+                dst = t[:].rearrange("p (c i) t -> p c t i", i=4)
+                src = raw[PIECES[i]].rearrange("p t (c i) -> p c t i", i=4)
+                if eng == "s":
+                    nc.scalar.copy(out=dst, in_=src)
+                else:
+                    nc.vector.tensor_copy(out=dst, in_=src)
             grouped[i] = t
 
         def quantize_blur(i):
-            g, h, c = PIECES[i]
+            g, c, h = PIECES[i]
             cols = slice(512 * g + 256 * h, 512 * g + 256 * (h + 1))
             nc.vector.quantize_mx(
                 out=bcodes[:, c, cols].bitcast(FP8X4),
@@ -106,230 +107,248 @@ def tile_weighted_lucy_ratio_g6_kernel(
                 in_=grouped[i][:].rearrange("p n t -> p (n t)"),
             )
 
-        def step_tiles(s, b):
-            g, ch, h = STEPS[s]
-            if h is None:
-                return [4 * g + 2 * b, 4 * g + 2 * b + 1]
-            return [4 * g + 2 * h + b]
-
         def product(s, b):
-            g, ch, h = STEPS[s]
-            m0, w = CHUNKS[ch]
+            g, r = divmod(s, CHUNKS)
+            rows = slice(W * r, W * (r + 1))
             if b == 0:
-                recip[s] = work.tile([P, 1024], F32, name="recip", tag="recip", bufs=3)
-            acc = psum.tile([P, 512], F32, name="acc", tag="acc", bufs=3)
-            for i, j in enumerate(step_tiles(s, b)):
+                recip[s] = work.tile([P, 4, W], F32, name="recip", tag="recip", bufs=3)
+            acc = psum.tile([P, 2, W], F32, name="acc", tag="acc", bufs=3)
+            for i in range(2):
+                cols = slice(512 * g + P * (2 * b + i), 512 * g + P * (2 * b + i + 1))
                 for c in range(PASSES):
                     nc.tensor.matmul_mx(
-                        out=acc[:, w * i : w * (i + 1)],
-                        lhsT=bcodes[:, c, P * j : P * (j + 1)].bitcast(FP8X4),
-                        lhsT_scale=bscales[:, c, P * j : P * (j + 1)],
-                        rhs=xw[:, c, m0 : m0 + w].bitcast(FP8X4),
-                        rhs_scale=xs[:, c, m0 : m0 + w],
+                        out=acc[:, i, :],
+                        lhsT=bcodes[:, c, cols].bitcast(FP8X4),
+                        lhsT_scale=bscales[:, c, cols],
+                        rhs=xw[:, c, rows].bitcast(FP8X4),
+                        rhs_scale=xs[:, c, rows],
                         start=(c == 0),
                         stop=(c == PASSES - 1),
                     )
-            for i, j in enumerate(step_tiles(s, b)):
+            for i in range(2):
+                j = 4 * g + 2 * b + i
                 nc.scalar.activation(
-                    out=recip[s][:, 512 * b + w * i : 512 * b + w * (i + 1)],
-                    in_=acc[:, w * i : w * (i + 1)],
+                    out=recip[s][:, 2 * b + i, :],
+                    in_=acc[:, i, :],
                     func=ACT.Abs_reciprocal_sqrt,
                     bias=bias[:, j : j + 1],
                     scale=inv_w[:, j : j + 1],
                 )
 
         def square(s, b):
-            half = recip[s][:, 512 * b : 512 * (b + 1)]
+            half = recip[s][:, 2 * b : 2 * b + 2, :]
             nc.scalar.activation(out=half, in_=half, func=ACT.Square)
 
-        def turn(s, b):
-            g, ch, h = STEPS[s]
-            m0, w = CHUNKS[ch]
-            bank = psum.tile([P, 512], F32, name="turned", tag="turned", bufs=3)
-            q = recip[s][:].rearrange("p (j m) -> p j m", m=w)
-            if h is None:
-                blocks = [(j, b) for j in range(4)]
+        def turn(s, a):
+            bank = psum.tile([P, 4, P], F32, name="turned", tag="turned", bufs=3)
+            for j in range(4):
+                nc.tensor.transpose(bank[:, j, :], recip[s][:, j, P * a : P * (a + 1)], ident[:])
+            turned[s, a] = bank
+
+        def multiply(s, a):
+            if a == 0:
+                ytile[s] = work.tile([P, 2, 512], F32, name="y", tag="y", bufs=9)
+            nc.vector.tensor_tensor(
+                out=ytile[s][:, a, :],
+                in0=turned[s, a][:].rearrange("m j n -> m (j n)"),
+                in1=meas[s][:, a, :],
+                op=ALU.mult,
+            )
+
+        def store_y(s, a0, a1):
+            g, r = divmod(s, CHUNKS)
+            dst = out_0[W * r + P * a0 : W * r + P * a1, 512 * g : 512 * (g + 1)]
+            nc.sync.dma_start(out=dst.rearrange("(a p) n -> p a n", p=P), in_=ytile[s][:, a0:a1, :])
+
+        def round_y(s, a0, a1, eng):
+            if a0 == 0:
+                ypairs[s] = work.tile([P, 2, 2, P, 2], BF16, name="ypairs", tag="ypairs", bufs=3)
+            dst = ypairs[s][:, a0:a1, :, :, :]
+            src = ytile[s][:, a0:a1, :].rearrange("m a (p u e) -> m a u p e", u=2, e=2)
+            if eng == "g":
+                nc.gpsimd.tensor_scalar(
+                    out=dst[:, 0], in0=src[:, 0], scalar1=1.0, scalar2=0.0, op0=ALU.mult, op1=ALU.add
+                )
+            elif eng == "s":
+                nc.scalar.copy(out=dst, in_=src)
             else:
-                blocks = [(j, 2 * b + a) for a in range(2) for j in range(2)]
-            for i, (j, a) in enumerate(blocks):
-                nc.tensor.transpose(bank[:, P * i : P * (i + 1)], q[:, j, P * a : P * (a + 1)], ident[:])
-            turned[s, b] = bank
+                nc.vector.tensor_copy(out=dst, in_=src)
 
-        def multiply(s, b):
-            g, ch, h = STEPS[s]
-            m0, w = CHUNKS[ch]
-            if b == 0 and h != 1:
-                ytile[g, ch] = work.tile([P, w // P, 512], F32, name="y", tag="y", bufs=6)
-            y = ytile[g, ch]
-            if h is None:
-                nc.vector.tensor_tensor(
-                    out=y[:, b, :], in0=turned[s, b][:], in1=meas[g, ch][:, b, :], op=ALU.mult
-                )
-            else:
-                rows = slice(2 * b, 2 * b + 2)
-                cols = slice(256 * h, 256 * (h + 1))
-                nc.vector.tensor_tensor(
-                    out=y[:, rows, cols],
-                    in0=turned[s, b][:].rearrange("p (a n) -> p a n", a=2),
-                    in1=meas[g, ch][:, rows, cols],
-                    op=ALU.mult,
-                )
+        def turn_pairs(s, a):
+            if a == 0:
+                pairs_ps[s] = psum.tile([P, 2, 2, P], F32, name="pairs", tag="pairs", bufs=2)
+            words = ypairs[s][:].rearrange("m a u p e -> m a u (p e)").bitcast(F32)
+            for u in range(2):
+                nc.tensor.transpose(pairs_ps[s][:, a, u, :], words[:, a, u, :], ident[:])
 
-        def store_y(s):
-            g, ch, h = STEPS[s]
-            m0, w = CHUNKS[ch]
-            dst = out_0[m0 : m0 + w, 512 * g : 512 * (g + 1)]
-            nc.sync.dma_start(out=dst.rearrange("(a p) n -> p a n", p=P), in_=ytile[g, ch][:])
-
-        def round_y(s):
-            g, ch, h = STEPS[s]
-            m0, w = CHUNKS[ch]
-            if h != 1:
-                ypairs[g, ch] = work.tile([P, w // P, 2, P, 2], BF16, name="ypairs", tag="ypairs", bufs=3)
-            dst = ypairs[g, ch]
-            y = ytile[g, ch]
-            if h is None:
-                nc.vector.tensor_copy(
-                    out=dst[:], in_=y[:].rearrange("m a (p u e) -> m a u p e", u=2, e=2)
-                )
-            else:
-                nc.vector.tensor_copy(
-                    out=dst[:, :, :, 64 * h : 64 * (h + 1), :],
-                    in_=y[:, :, 256 * h : 256 * (h + 1)].rearrange("m a (p u e) -> m a u p e", u=2, e=2),
-                )
-
-        def turn_pairs(k):
-            g, r = divmod(k, 5)
-            words = ypairs[g, r // 2][:].rearrange("m a u p e -> m a u (p e)").bitcast(F32)
-            bank = psum.tile([P, 2, 2, P], F32, name="pairs", tag="pairs", bufs=2)
-            for a in range(2):
-                for u in range(2):
-                    nc.tensor.transpose(bank[:, a, u, :], words[:, 2 * (r % 2) + a, u, :], ident[:])
-            pairs_ps[k] = bank
-
-        def gather_quads(k, on_scalar):
+        def gather_quads(s, on_scalar):
             t = work.tile([P, 1024], BF16, name="yquads", tag="yquads", bufs=3, align_bytes=64)
             dst = t[:].bitcast(F32).rearrange("p (a m u) -> p a m u", a=2, u=2)
-            src = pairs_ps[k][:].rearrange("p a u m -> p a m u")
+            src = pairs_ps[s][:].rearrange("p a u m -> p a m u")
             if on_scalar:
                 nc.scalar.copy(out=dst, in_=src)
             else:
                 nc.vector.tensor_copy(out=dst, in_=src)
-            yquads[k] = t
+            yquads[s] = t
 
-        def quantize_y(k):
-            g, r = divmod(k, 5)
-            cols = slice(256 * r, 256 * (r + 1))
+        def quantize_y(s):
+            g, r = divmod(s, CHUNKS)
+            cols = slice(W * r, W * (r + 1))
             nc.vector.quantize_mx(
-                out=ycodes[:, g, cols].bitcast(FP8X4), scales=yscales[:, g, cols], in_=yquads[k][:]
+                out=ycodes[:, g, cols].bitcast(FP8X4), scales=yscales[:, g, cols], in_=yquads[s][:]
             )
 
         def store_codes(g, m0, m1):
             dst = out_1[g].rearrange("p m t -> p (m t)")[:, 4 * m0 : 4 * m1]
             nc.sync.dma_start(out=dst.bitcast(I32), in_=ycodes[:, g, m0:m1].bitcast(I32))
 
-        def store_scales(g0, g1):
+        def store_scales(g0, g1, eng):
             for quad in range(4):
                 dst = out_2[g0:g1, 4 * quad : 4 * quad + 4, :].rearrange("g r m -> r g m")
-                nc.sync.dma_start(
+                eng.dma_start(
                     out=dst.bitcast(I32), in_=yscales[32 * quad : 32 * quad + 4, g0:g1, :].bitcast(I32)
                 )
 
-        nc.vector.memset(one[:], 1.0)
-        nc.scalar.activation(out=warm[:], in_=one[:], func=ACT.Abs_reciprocal_sqrt)
         nc.vector.memset(xs[:].bitcast(I32), 0)
+        nc.vector.memset(one[:], 1.0)
+        nc.gpsimd.dma_start(out=vec_rows[0:16, :], in_=background.rearrange("(j p) -> j p", p=P))
+        nc.gpsimd.dma_start(out=vec_rows[16:32, :], in_=weight.rearrange("(j p) -> j p", p=P))
         make_identity(nc, ident[:])
         nc.gpsimd.memset(vec_wide[:], 0.0)
-        for c in range(PASSES):
-            load_blur(0, c, 0)
+        load_blur(0, 0, 1)
+        load_blur(0, 1, 1)
+        load_blur(0, 2, 1)
+        load_x(0, 1)
         for quad in range(4):
             src = x_scales[:, 4 * quad : 4 * quad + 4, :].rearrange("c r m -> r c m")
-            nc.sync.dma_start(out=xs[32 * quad : 32 * quad + 4, :, :].bitcast(I32), in_=src.bitcast(I32))
-        nc.sync.dma_start(out=vec_rows[0:16, :], in_=background.rearrange("(j p) -> j p", p=P))
-        nc.sync.dma_start(out=vec_rows[16:32, :], in_=weight.rearrange("(j p) -> j p", p=P))
-        load_x(0)
-        for c in range(PASSES):
-            load_blur(0, c, 1)
-        load_meas(0, 0)
-        load_x(1)
-        for c in range(PASSES):
-            load_blur(1, c, None)
-        load_meas(0, 1)
-        load_x(2)
-        load_meas(0, 2)
-        for c in range(PASSES):
-            load_blur(2, c, None)
-        load_meas(1, 0)
+            nc.scalar.dma_start(out=xs[32 * quad : 32 * quad + 4, :, :].bitcast(I32), in_=src.bitcast(I32))
+        nc.scalar.activation(out=warm[:], in_=one[:], func=ACT.Abs_reciprocal_sqrt)
+        load_x(1, 2)
+        load_blur(1, 0, 1)
+        load_meas(0, 0, 1, 2)
+        load_x(2, 3)
+        load_blur(1, 1, 1)
+        load_x(3, 4)
+        load_meas(0, 2, 1, 2)
+        load_blur(1, 2, 1)
+        load_x(4, 5)
+        load_blur(2, 0, 2)
+        load_meas(0, 4, 1, 1)
+        load_meas(1, 0, 1, 2)
+        load_blur(2, 1, 2)
+        load_blur(2, 2, 2)
+        load_meas(1, 2, 1, 2)
+        load_meas(1, 4, 1, 1)
 
-        interleave(0, False)
-        interleave(1, True)
-        interleave(2, False)
-        quantize_blur(0)
+        interleave(0, "v")
+        interleave(1, "s")
         nc.vector.tensor_copy(out=vec_wide[0:32, :], in_=vec_rows[:])
-        quantize_blur(1)
+        quantize_blur(0)
         vec_ps = psum.tile([P, 2, 2, P], F32, name="pairs", tag="pairs", bufs=2)
         nc.tensor.transpose(vec_ps[:, 0, 0, :], vec_wide[:], ident[:])
-        quantize_blur(2)
+        interleave(2, "v")
+        interleave(3, "s")
+        quantize_blur(1)
         nc.vector.reciprocal(out=inv_w[:], in_=vec_ps[:, 0, 0, 16:32])
+        quantize_blur(2)
         nc.vector.tensor_tensor(out=bias[:], in0=vec_ps[:, 0, 0, 0:16], in1=inv_w[:], op=ALU.mult)
+        interleave(4, "v")
+        interleave(5, "s")
+        quantize_blur(3)
+        quantize_blur(4)
+        quantize_blur(5)
 
-        vector_pieces = {0: [3, 4, 5], 2: [6, 7], 3: [9], 15: [22, 23]}
-        for s in range(4, 15):
-            vector_pieces[s] = [s + 7]
-        scalar_pieces = {2: [8], 3: [10]}
-        meas_loads = {5 * g + 2 * ch + 1 - 4: (g, ch) for g in range(GROUPS) for ch in range(3)}
+        vector_pieces = {1: [6, 7], 4: [11]}
+        scalar_pieces = {3: [10], 7: [16], 12: [22]}
+        pool_pieces = {2: [8], 3: [9], 4: [12], 5: [13], 6: [14], 7: [15], 8: [17], 9: [18], 10: [19], 11: [20], 12: [21], 13: [23]}
+        scalar_gathers = (4, 5, 9, 10)
+        dmas = {1: [("y", 0)], 2: [("y", 1)], 3: [("y", 2)], 4: [("y", 3)], 5: [("y", 4), ("m", 2, 0, 2, 1)], 6: [("y", 5), ("m", 2, 1, 2, 1)], 7: [("y", 6), ("m", 2, 2, 2, 1)], 8: [("y", 7), ("m", 2, 3, 2, 1), ("c", 0, 0, M)], 9: [("y", 8), ("m", 2, 4, 2, 1)], 10: [("y", 9)], 11: [("y", 10)], 12: [("y", 11)], 13: [("y", 12), ("c", 1, 0, M), ("s", 0, 2)], 14: [("y", 13)], 15: [("y", 14)], 16: [("y", 15)], 17: [("y", 16)], 18: [("y", 17), ("c", 2, 0, M), ("s", 2, 3)], 19: [("y", 18)]}
+
+        def live(s):
+            return 0 <= s < NSTEP
 
         pending = []
-        for s in range(NSTEP + 5):
-            if s >= 3 and s in meas_loads:
-                load_meas(*meas_loads[s])
-            if 6 <= s <= 8:
-                load_blur(3, s - 6, None)
-            if s < NSTEP:
-                product(s, 0)
+        for s in range(NSTEP):
+            product(s, 0)
             mine = vector_pieces.get(s, [])
             for i in mine[:1]:
-                interleave(i, False)
-            if 0 <= s - 5 < NSTEP and not mine:
-                quantize_y(s - 5)
-            if 0 <= s - 2 < NSTEP:
-                round_y(s - 2)
-            if 0 <= s - 5 < NSTEP and mine:
-                quantize_y(s - 5)
+                interleave(i, "v")
+            if not mine and live(s - 4):
+                quantize_y(s - 4)
+            if live(s - 2):
+                round_y(s - 2, 0, 2, "v")
+            if mine and live(s - 4):
+                quantize_y(s - 4)
+            for n, i in enumerate(mine):
+                if n + 1 < len(mine):
+                    interleave(mine[n + 1], "v")
+                quantize_blur(i)
             for i in pending:
                 quantize_blur(i)
             pending = []
-            for n, i in enumerate(mine):
-                if n + 1 < len(mine):
-                    interleave(mine[n + 1], False)
-                quantize_blur(i)
-            if s < NSTEP:
-                product(s, 1)
-                square(s, 0)
-            if 0 <= s - 1 < NSTEP:
+            for i in pool_pieces.get(s, []):
+                interleave(i, "g")
+                pending.append(i)
+            if live(s - 3) and s in scalar_gathers:
+                gather_quads(s - 3, True)
+            product(s, 1)
+            square(s, 0)
+            if live(s - 1):
                 turn(s - 1, 0)
                 turn(s - 1, 1)
-            if 0 <= s - 3 < NSTEP:
-                turn_pairs(s - 3)
+            if live(s - 2):
+                turn_pairs(s - 2, 0)
+                turn_pairs(s - 2, 1)
             for i in scalar_pieces.get(s, []):
-                interleave(i, True)
-                pending.append(i)
-            if 0 <= s - 4 < NSTEP:
-                gather_quads(s - 4, s < 17)
-            if s < NSTEP:
-                square(s, 1)
-            if 0 <= s - 1 < NSTEP:
+                interleave(i, "s")
+                pending.insert(0, i)
+            if live(s - 3) and s not in scalar_gathers:
+                gather_quads(s - 3, False)
+            square(s, 1)
+            if live(s - 1):
                 multiply(s - 1, 0)
                 multiply(s - 1, 1)
-                if STEPS[s - 1][2] != 0:
-                    store_y(s - 1)
-            k = s - 5
-            if k in (4, 9, 14):
-                store_codes(k // 5, 0, M)
-            if k == 14:
-                store_scales(0, 3)
-            if k == 18:
-                store_codes(3, 0, 1024)
-            if k == 19:
-                store_codes(3, 1024, M)
-                store_scales(3, 4)
+            for d in dmas.get(s, []):
+                if d[0] == "y":
+                    store_y(d[1], 0, 2)
+                elif d[0] == "m":
+                    load_meas(*d[1:])
+                elif d[0] == "b":
+                    load_blur(*d[1:])
+                elif d[0] == "c":
+                    store_codes(*d[1:])
+                else:
+                    store_scales(d[1], d[2], nc.sync)
+
+        last = NSTEP - 1
+        quantize_y(last - 3)
+        round_y(last - 1, 0, 2, "v")
+        gather_quads(last - 2, True)
+        turn(last, 0)
+        turn(last, 1)
+        turn_pairs(last - 1, 0)
+        turn_pairs(last - 1, 1)
+        multiply(last, 0)
+        store_y(last, 0, 1)
+        round_y(last, 0, 1, "s")
+        gather_quads(last - 1, True)
+        multiply(last, 1)
+        store_y(last, 1, 2)
+        quantize_y(last - 2)
+        round_y(last, 1, 2, "v")
+        quantize_y(last - 1)
+        store_codes(3, 0, 1024)
+        words = ypairs[last][:].rearrange("m a u p e -> m a u (p e)").bitcast(F32)
+        yquads[last] = work.tile([P, 1024], BF16, name="yquads", tag="yquads", bufs=3, align_bytes=64)
+        quads = yquads[last][:].bitcast(F32).rearrange("p (a m u) -> p a m u", a=2, u=2)
+        for a in range(2):
+            bank = psum.tile([P, 2, P], F32, name="acc", tag="acc", bufs=3)
+            for u in range(2):
+                nc.tensor.transpose(bank[:, u, :], words[:, a, u, :], ident[:])
+            if a == 0:
+                nc.scalar.copy(out=quads[:, a], in_=bank[:].rearrange("p u m -> p m u"))
+            else:
+                nc.vector.tensor_copy(out=quads[:, a], in_=bank[:].rearrange("p u m -> p m u"))
+        quantize_y(last)
+        store_codes(3, 1024, M)
+        store_scales(3, 4, nc.scalar)

@@ -209,12 +209,13 @@ def tile_weighted_lucy_ratio_g6_kernel(
                     out=dst.bitcast(I32), in_=yscales[32 * quad : 32 * quad + 4, g0:g1, :].bitcast(I32)
                 )
 
-        nc.vector.memset(xs[:].bitcast(I32), 0)
         nc.vector.memset(one[:], 1.0)
-        nc.gpsimd.dma_start(out=vec_rows[0:16, :], in_=background.rearrange("(j p) -> j p", p=P))
-        nc.gpsimd.dma_start(out=vec_rows[16:32, :], in_=weight.rearrange("(j p) -> j p", p=P))
+        nc.vector.memset(xs[:].bitcast(I32), 0)
+        nc.scalar.activation(out=warm[:], in_=one[:], func=ACT.Abs_reciprocal_sqrt)
         make_identity(nc, ident[:])
         nc.gpsimd.memset(vec_wide[:], 0.0)
+        nc.sync.dma_start(out=vec_rows[0:16, :], in_=background.rearrange("(j p) -> j p", p=P))
+        nc.sync.dma_start(out=vec_rows[16:32, :], in_=weight.rearrange("(j p) -> j p", p=P))
         load_blur(0, 0, 1)
         load_blur(0, 1, 1)
         load_blur(0, 2, 1)
@@ -222,7 +223,6 @@ def tile_weighted_lucy_ratio_g6_kernel(
         for quad in range(4):
             src = x_scales[:, 4 * quad : 4 * quad + 4, :].rearrange("c r m -> r c m")
             nc.scalar.dma_start(out=xs[32 * quad : 32 * quad + 4, :, :].bitcast(I32), in_=src.bitcast(I32))
-        nc.scalar.activation(out=warm[:], in_=one[:], func=ACT.Abs_reciprocal_sqrt)
         load_x(1, 2)
         load_blur(1, 0, 1)
         load_meas(0, 0, 1, 2)
@@ -240,23 +240,20 @@ def tile_weighted_lucy_ratio_g6_kernel(
         load_meas(1, 2, 1, 2)
         load_meas(1, 4, 1, 1)
 
+        nc.vector.tensor_copy(out=vec_wide[0:32, :], in_=vec_rows[:])
+        vec_ps = psum.tile([P, P], F32, name="vec_ps", tag="pairs", bufs=2)
+        nc.tensor.transpose(vec_ps[:], vec_wide[:], ident[:])
+        nc.vector.reciprocal(out=inv_w[:], in_=vec_ps[:, 16:32])
         interleave(0, "v")
         interleave(1, "s")
-        nc.vector.tensor_copy(out=vec_wide[0:32, :], in_=vec_rows[:])
+        nc.vector.tensor_tensor(out=bias[:], in0=vec_ps[:, 0:16], in1=inv_w[:], op=ALU.mult)
         quantize_blur(0)
-        vec_ps = psum.tile([P, 2, 2, P], F32, name="pairs", tag="pairs", bufs=2)
-        nc.tensor.transpose(vec_ps[:, 0, 0, :], vec_wide[:], ident[:])
-        interleave(2, "v")
-        interleave(3, "s")
-        quantize_blur(1)
-        nc.vector.reciprocal(out=inv_w[:], in_=vec_ps[:, 0, 0, 16:32])
-        quantize_blur(2)
-        nc.vector.tensor_tensor(out=bias[:], in0=vec_ps[:, 0, 0, 0:16], in1=inv_w[:], op=ALU.mult)
-        interleave(4, "v")
-        interleave(5, "s")
-        quantize_blur(3)
-        quantize_blur(4)
-        quantize_blur(5)
+        for c in range(1, PASSES):
+            interleave(2 * c, "v")
+            interleave(2 * c + 1, "s")
+            quantize_blur(2 * c - 1)
+            quantize_blur(2 * c)
+        quantize_blur(2 * PASSES - 1)
 
         vector_pieces = {1: [6, 7], 4: [11]}
         scalar_pieces = {3: [10], 7: [16], 12: [22]}

@@ -54,6 +54,7 @@ def tile_weighted_lucy_ratio_g6_kernel(
         recip = {}
         turned = {}
         ytile = {}
+        wide = {}
         ypairs = {}
         pairs_ps = {}
         yquads = {}
@@ -70,7 +71,7 @@ def tile_weighted_lucy_ratio_g6_kernel(
             nc.sync.dma_start(out=xw[:, :, W * r0 : W * r1].bitcast(I32), in_=src.bitcast(I32))
 
         def load_meas(g, r, ng, nr):
-            t = work.tile([P, 2 * nr, 512 * ng], BF16, name="meas", tag="meas", bufs=8)
+            t = work.tile([P, 2 * nr, 512 * ng], BF16, name="meas", tag="meas", bufs=6)
             src = measured[W * r : W * (r + nr), 512 * g : 512 * (g + ng)]
             nc.sync.dma_start(out=t[:], in_=src.rearrange("(a p) n -> p a n", p=P))
             for i in range(ng):
@@ -146,8 +147,12 @@ def tile_weighted_lucy_ratio_g6_kernel(
             turned[s, a] = bank
 
         def multiply(s, a):
-            if a == 0:
-                ytile[s] = work.tile([P, 2, 512], F32, name="y", tag="y", bufs=9)
+            if a == 0 and s < CHUNKS:
+                wide[s] = work.tile([P, 2, 1024], F32, name="y", tag="y", bufs=6)
+                ytile[s] = wide[s][:, :, 0:512]
+                ytile[s + CHUNKS] = wide[s][:, :, 512:1024]
+            elif a == 0 and s >= 2 * CHUNKS:
+                ytile[s] = work.tile([P, 2, 512], F32, name="y", tag="y", bufs=6)
             nc.vector.tensor_tensor(
                 out=ytile[s][:, a, :],
                 in0=turned[s, a][:].rearrange("m j n -> m (j n)"),
@@ -214,9 +219,9 @@ def tile_weighted_lucy_ratio_g6_kernel(
         nc.scalar.activation(out=warm[:], in_=one[:], func=ACT.Abs_reciprocal_sqrt)
         make_identity(nc, ident[:])
         nc.gpsimd.memset(vec_wide[:], 0.0)
+        load_blur(0, 0, 1)
         nc.sync.dma_start(out=vec_rows[0:16, :], in_=background.rearrange("(j p) -> j p", p=P))
         nc.sync.dma_start(out=vec_rows[16:32, :], in_=weight.rearrange("(j p) -> j p", p=P))
-        load_blur(0, 0, 1)
         load_blur(0, 1, 1)
         load_blur(0, 2, 1)
         load_x(0, 1)
@@ -239,15 +244,17 @@ def tile_weighted_lucy_ratio_g6_kernel(
         load_blur(2, 2, 2)
         load_meas(1, 2, 1, 2)
         load_meas(1, 4, 1, 1)
+        load_meas(2, 0, 2, 1)
+        load_meas(2, 1, 2, 1)
 
+        interleave(0, "v")
+        interleave(1, "s")
         nc.vector.tensor_copy(out=vec_wide[0:32, :], in_=vec_rows[:])
         vec_ps = psum.tile([P, P], F32, name="vec_ps", tag="pairs", bufs=2)
         nc.tensor.transpose(vec_ps[:], vec_wide[:], ident[:])
-        nc.vector.reciprocal(out=inv_w[:], in_=vec_ps[:, 16:32])
-        interleave(0, "v")
-        interleave(1, "s")
-        nc.vector.tensor_tensor(out=bias[:], in0=vec_ps[:, 0:16], in1=inv_w[:], op=ALU.mult)
         quantize_blur(0)
+        nc.vector.reciprocal(out=inv_w[:], in_=vec_ps[:, 16:32])
+        nc.vector.tensor_tensor(out=bias[:], in0=vec_ps[:, 0:16], in1=inv_w[:], op=ALU.mult)
         for c in range(1, PASSES):
             interleave(2 * c, "v")
             interleave(2 * c + 1, "s")
@@ -258,8 +265,8 @@ def tile_weighted_lucy_ratio_g6_kernel(
         vector_pieces = {1: [6, 7], 4: [11]}
         scalar_pieces = {3: [10], 7: [16], 12: [22]}
         pool_pieces = {2: [8], 3: [9], 4: [12], 5: [13], 6: [14], 7: [15], 8: [17], 9: [18], 10: [19], 11: [20], 12: [21], 13: [23]}
-        scalar_gathers = (4, 5, 9, 10)
-        dmas = {1: [("y", 0)], 2: [("y", 1)], 3: [("y", 2)], 4: [("y", 3)], 5: [("y", 4), ("m", 2, 0, 2, 1)], 6: [("y", 5), ("m", 2, 1, 2, 1)], 7: [("y", 6), ("m", 2, 2, 2, 1)], 8: [("y", 7), ("m", 2, 3, 2, 1), ("c", 0, 0, M)], 9: [("y", 8), ("m", 2, 4, 2, 1)], 10: [("y", 9)], 11: [("y", 10)], 12: [("y", 11)], 13: [("y", 12), ("c", 1, 0, M), ("s", 0, 2)], 14: [("y", 13)], 15: [("y", 14)], 16: [("y", 15)], 17: [("y", 16)], 18: [("y", 17), ("c", 2, 0, M), ("s", 2, 3)], 19: [("y", 18)]}
+        scalar_gathers = (5, 10)
+        dmas = {6: [("w", 0), ("m", 2, 2, 2, 1)], 7: [("w", 1)], 8: [("w", 2), ("m", 2, 3, 2, 1), ("c", 0, 0, M)], 9: [("w", 3), ("m", 2, 4, 2, 1)], 10: [("w", 4)], 11: [("y", 10)], 12: [("y", 11)], 13: [("y", 12), ("c", 1, 0, M), ("s", 0, 2)], 14: [("y", 13)], 15: [("y", 14)], 16: [("y", 15)], 17: [("y", 16)], 18: [("y", 17), ("c", 2, 0, M), ("s", 2, 3)], 19: [("y", 18)]}
 
         def live(s):
             return 0 <= s < NSTEP
@@ -306,7 +313,10 @@ def tile_weighted_lucy_ratio_g6_kernel(
                 multiply(s - 1, 0)
                 multiply(s - 1, 1)
             for d in dmas.get(s, []):
-                if d[0] == "y":
+                if d[0] == "w":
+                    dst = out_0[W * d[1] : W * (d[1] + 1), 0:1024]
+                    nc.sync.dma_start(out=dst.rearrange("(a p) n -> p a n", p=P), in_=wide[d[1]][:])
+                elif d[0] == "y":
                     store_y(d[1], 0, 2)
                 elif d[0] == "m":
                     load_meas(*d[1:])
@@ -320,6 +330,7 @@ def tile_weighted_lucy_ratio_g6_kernel(
         last = NSTEP - 1
         quantize_y(last - 3)
         round_y(last - 1, 0, 2, "v")
+        store_codes(3, 0, 512)
         gather_quads(last - 2, True)
         turn(last, 0)
         turn(last, 1)
@@ -334,7 +345,7 @@ def tile_weighted_lucy_ratio_g6_kernel(
         quantize_y(last - 2)
         round_y(last, 1, 2, "v")
         quantize_y(last - 1)
-        store_codes(3, 0, 1024)
+        store_codes(3, 512, 1024)
         words = ypairs[last][:].rearrange("m a u p e -> m a u (p e)").bitcast(F32)
         yquads[last] = work.tile([P, 1024], BF16, name="yquads", tag="yquads", bufs=3, align_bytes=64)
         quads = yquads[last][:].bitcast(F32).rearrange("p (a m u) -> p a m u", a=2, u=2)

from contextlib import ExitStack

import concourse.mybir as mybir
from concourse.masks import make_identity

M, K, N = 1280, 1536, 2048
FLOPS = 2 * M * K * N

F32 = mybir.dt.float32
BF16 = mybir.dt.bfloat16
I32 = mybir.dt.int32
U32 = mybir.dt.uint32
U8 = mybir.dt.uint8
FP8X4 = mybir.dt.float8_e4m3fn_x4
ACT = mybir.ActivationFunctionType
ALU = mybir.AluOpType

P = 128
PASSES = K // 512
GROUPS = N // 512
W = 256
CHUNKS = M // W
NSTEP = GROUPS * CHUNKS
PIECES = [(g, c, h) for g in range(GROUPS) for c in range(PASSES) for h in range(2)]


def tile_weighted_lucy_ratio_g6_kernel(
    tc, x_words, x_scales, blur, measured, background, weight, out_0, out_1, out_2
):
    nc = tc.nc
    with ExitStack() as ctx:
        keep = ctx.enter_context(tc.tile_pool(name="keep", bufs=1))
        work = ctx.enter_context(tc.tile_pool(name="work", bufs=3))
        psum = ctx.enter_context(tc.psum_pool(name="psum", bufs=3))
        ctx.enter_context(tc.manual_schedule())

        xw = keep.tile([P, PASSES, M], U32, align_bytes=64)
        xs = keep.tile([P, PASSES, M], U8, align_bytes=64)
        bcodes = keep.tile([P, PASSES, N], U32, align_bytes=64)
        bscales = keep.tile([P, PASSES, N], U8, align_bytes=64)
        ycodes = keep.tile([P, GROUPS, M], U32, align_bytes=64)
        yscales = keep.tile([P, GROUPS, M], U8, align_bytes=64)
        ident = keep.tile([P, P], F32)
        vec_rows = keep.tile([32, P], BF16)
        vec_wide = keep.tile([P, P], F32)
        inv_w = keep.tile([P, 16], F32)
        bias = keep.tile([P, 16], F32)
        one = keep.tile([P, 1], F32)
        warm = keep.tile([P, 1], F32)

        raw = {}
        grouped = {}
        meas = {}
        recip = {}
        turned = {}
        ytile = {}
        wide = {}
        ypairs = {}
        pairs_ps = {}
        yquads = {}

        def load_blur(g, c, ng):
            rows = blur[512 * c : 512 * (c + 1), :].rearrange("(p t) n -> p t n", t=4)
            t = work.tile([P, 4, 512 * ng], BF16, name="raw%d" % ng, tag="raw%d" % ng, bufs=6 // ng)
            nc.sync.dma_start(out=t[:], in_=rows[:, :, 512 * g : 512 * (g + ng)])
            for i in range(2 * ng):
                raw[g + i // 2, c, i % 2] = t[:, :, 256 * i : 256 * (i + 1)]

        def load_x(r0, r1):
            src = x_words.rearrange("c p m t -> p c (m t)")[:, :, 4 * W * r0 : 4 * W * r1]
            nc.sync.dma_start(out=xw[:, :, W * r0 : W * r1].bitcast(I32), in_=src.bitcast(I32))

        def load_meas(g, r, ng, nr):
            t = work.tile([P, 2 * nr, 512 * ng], BF16, name="meas", tag="meas", bufs=6)
            src = measured[W * r : W * (r + nr), 512 * g : 512 * (g + ng)]
            nc.sync.dma_start(out=t[:], in_=src.rearrange("(a p) n -> p a n", p=P))
            for i in range(ng):
                for j in range(nr):
                    meas[CHUNKS * (g + i) + r + j] = t[:, 2 * j : 2 * j + 2, 512 * i : 512 * (i + 1)]

        def interleave(i, eng):
            if eng == "g":
                t = work.tile([P, 256, 4], BF16, name="slow", tag="slow", bufs=1, align_bytes=64)
                nc.gpsimd.tensor_scalar(
                    out=t[:],
                    in0=raw[PIECES[i]].rearrange("p t n -> p n t"),
                    scalar1=1.0,
                    scalar2=0.0,
                    op0=ALU.mult,
                    op1=ALU.add,
                )
            else:
                t = work.tile([P, 256, 4], BF16, name="grouped", tag="grouped", bufs=4, align_bytes=64)
                dst = t[:].rearrange("p (c i) t -> p c t i", i=4)
                src = raw[PIECES[i]].rearrange("p t (c i) -> p c t i", i=4)
                if eng == "s":
                    nc.scalar.copy(out=dst, in_=src)
                else:
                    nc.vector.tensor_copy(out=dst, in_=src)
            grouped[i] = t

        def quantize_blur(i):
            g, c, h = PIECES[i]
            cols = slice(512 * g + 256 * h, 512 * g + 256 * (h + 1))
            nc.vector.quantize_mx(
                out=bcodes[:, c, cols].bitcast(FP8X4),
                scales=bscales[:, c, cols],
                in_=grouped[i][:].rearrange("p n t -> p (n t)"),
            )

        def product(s, b):
            g, r = divmod(s, CHUNKS)
            rows = slice(W * r, W * (r + 1))
            if b == 0:
                recip[s] = work.tile([P, 4, W], F32, name="recip", tag="recip", bufs=3)
            acc = psum.tile([P, 2, W], F32, name="acc", tag="acc", bufs=3)
            for i in range(2):
                cols = slice(512 * g + P * (2 * b + i), 512 * g + P * (2 * b + i + 1))
                for c in range(PASSES):
                    nc.tensor.matmul_mx(
                        out=acc[:, i, :],
                        lhsT=bcodes[:, c, cols].bitcast(FP8X4),
                        lhsT_scale=bscales[:, c, cols],
                        rhs=xw[:, c, rows].bitcast(FP8X4),
                        rhs_scale=xs[:, c, rows],
                        start=(c == 0),
                        stop=(c == PASSES - 1),
                    )
            for i in range(2):
                j = 4 * g + 2 * b + i
                nc.scalar.activation(
                    out=recip[s][:, 2 * b + i, :],
                    in_=acc[:, i, :],
                    func=ACT.Abs_reciprocal_sqrt,
                    bias=bias[:, j : j + 1],
                    scale=inv_w[:, j : j + 1],
                )

        def square(s, b):
            half = recip[s][:, 2 * b : 2 * b + 2, :]
            nc.scalar.activation(out=half, in_=half, func=ACT.Square)

        def turn(s, a):
            bank = psum.tile([P, 4, P], F32, name="turned", tag="turned", bufs=3)
            for j in range(4):
                nc.tensor.transpose(bank[:, j, :], recip[s][:, j, P * a : P * (a + 1)], ident[:])
            turned[s, a] = bank

        def multiply(s, a):
            if a == 0 and s < CHUNKS:
                wide[s] = work.tile([P, 2, 1024], F32, name="y", tag="y", bufs=6)
                ytile[s] = wide[s][:, :, 0:512]
                ytile[s + CHUNKS] = wide[s][:, :, 512:1024]
            elif a == 0 and s >= 2 * CHUNKS:
                ytile[s] = work.tile([P, 2, 512], F32, name="y", tag="y", bufs=6)
            nc.vector.tensor_tensor(
                out=ytile[s][:, a, :],
                in0=turned[s, a][:].rearrange("m j n -> m (j n)"),
                in1=meas[s][:, a, :],
                op=ALU.mult,
            )

        def store_y(s, a0, a1):
            g, r = divmod(s, CHUNKS)
            dst = out_0[W * r + P * a0 : W * r + P * a1, 512 * g : 512 * (g + 1)]
            nc.sync.dma_start(out=dst.rearrange("(a p) n -> p a n", p=P), in_=ytile[s][:, a0:a1, :])

        def round_y(s, a0, a1, eng):
            if a0 == 0:
                ypairs[s] = work.tile([P, 2, 2, P, 2], BF16, name="ypairs", tag="ypairs", bufs=3)
            dst = ypairs[s][:, a0:a1, :, :, :]
            src = ytile[s][:, a0:a1, :].rearrange("m a (p u e) -> m a u p e", u=2, e=2)
            if eng == "g":
                nc.gpsimd.tensor_scalar(
                    out=dst[:, 0], in0=src[:, 0], scalar1=1.0, scalar2=0.0, op0=ALU.mult, op1=ALU.add
                )
            elif eng == "s":
                nc.scalar.copy(out=dst, in_=src)
            else:
                nc.vector.tensor_copy(out=dst, in_=src)

        def turn_pairs(s, a):
            if a == 0:
                pairs_ps[s] = psum.tile([P, 2, 2, P], F32, name="pairs", tag="pairs", bufs=2)
            words = ypairs[s][:].rearrange("m a u p e -> m a u (p e)").bitcast(F32)
            for u in range(2):
                nc.tensor.transpose(pairs_ps[s][:, a, u, :], words[:, a, u, :], ident[:])

        def gather_quads(s, on_scalar):
            t = work.tile([P, 1024], BF16, name="yquads", tag="yquads", bufs=3, align_bytes=64)
            dst = t[:].bitcast(F32).rearrange("p (a m u) -> p a m u", a=2, u=2)
            src = pairs_ps[s][:].rearrange("p a u m -> p a m u")
            if on_scalar:
                nc.scalar.copy(out=dst, in_=src)
            else:
                nc.vector.tensor_copy(out=dst, in_=src)
            yquads[s] = t

        def quantize_y(s):
            g, r = divmod(s, CHUNKS)
            cols = slice(W * r, W * (r + 1))
            nc.vector.quantize_mx(
                out=ycodes[:, g, cols].bitcast(FP8X4), scales=yscales[:, g, cols], in_=yquads[s][:]
            )

        def store_codes(g, m0, m1):
            dst = out_1[g].rearrange("p m t -> p (m t)")[:, 4 * m0 : 4 * m1]
            nc.sync.dma_start(out=dst.bitcast(I32), in_=ycodes[:, g, m0:m1].bitcast(I32))

        def store_scales(g0, g1, eng):
            for quad in range(4):
                dst = out_2[g0:g1, 4 * quad : 4 * quad + 4, :].rearrange("g r m -> r g m")
                eng.dma_start(
                    out=dst.bitcast(I32), in_=yscales[32 * quad : 32 * quad + 4, g0:g1, :].bitcast(I32)
                )

        nc.vector.memset(one[:], 1.0)
        nc.vector.memset(xs[:].bitcast(I32), 0)
        nc.scalar.activation(out=warm[:], in_=one[:], func=ACT.Abs_reciprocal_sqrt)
        make_identity(nc, ident[:])
        nc.gpsimd.memset(vec_wide[:], 0.0)
        load_blur(0, 0, 1)
        nc.sync.dma_start(out=vec_rows[0:16, :], in_=background.rearrange("(j p) -> j p", p=P))
        nc.sync.dma_start(out=vec_rows[16:32, :], in_=weight.rearrange("(j p) -> j p", p=P))
        load_blur(0, 1, 1)
        load_blur(0, 2, 1)
        load_x(0, 1)
        for quad in range(4):
            src = x_scales[:, 4 * quad : 4 * quad + 4, :].rearrange("c r m -> r c m")
            nc.scalar.dma_start(out=xs[32 * quad : 32 * quad + 4, :, :].bitcast(I32), in_=src.bitcast(I32))
        load_x(1, 2)
        load_blur(1, 0, 1)
        load_meas(0, 0, 1, 2)
        load_x(2, 3)
        load_blur(1, 1, 1)
        load_x(3, 4)
        load_meas(0, 2, 1, 2)
        load_blur(1, 2, 1)
        load_x(4, 5)
        load_blur(2, 0, 2)
        load_meas(0, 4, 1, 1)
        load_meas(1, 0, 1, 2)
        load_blur(2, 1, 2)
        load_blur(2, 2, 2)
        load_meas(1, 2, 1, 2)
        load_meas(1, 4, 1, 1)
        load_meas(2, 0, 2, 1)
        load_meas(2, 1, 2, 1)

        interleave(0, "v")
        interleave(1, "s")
        nc.vector.tensor_copy(out=vec_wide[0:32, :], in_=vec_rows[:])
        vec_ps = psum.tile([P, P], F32, name="vec_ps", tag="pairs", bufs=2)
        nc.tensor.transpose(vec_ps[:], vec_wide[:], ident[:])
        quantize_blur(0)
        nc.vector.reciprocal(out=inv_w[:], in_=vec_ps[:, 16:32])
        nc.vector.tensor_tensor(out=bias[:], in0=vec_ps[:, 0:16], in1=inv_w[:], op=ALU.mult)
        for c in range(1, PASSES):
            interleave(2 * c, "v")
            interleave(2 * c + 1, "s")
            quantize_blur(2 * c - 1)
            quantize_blur(2 * c)
        quantize_blur(2 * PASSES - 1)

        vector_pieces = {1: [6, 7], 4: [11]}
        scalar_pieces = {3: [10], 7: [16], 12: [22]}
        pool_pieces = {2: [8], 3: [9], 4: [12], 5: [13], 6: [14], 7: [15], 8: [17], 9: [18], 10: [19], 11: [20], 12: [21], 13: [23]}
        scalar_gathers = (5, 10)
        dmas = {6: [("w", 0), ("m", 2, 2, 2, 1)], 7: [("w", 1)], 8: [("w", 2), ("m", 2, 3, 2, 1), ("c", 0, 0, M)], 9: [("w", 3), ("m", 2, 4, 2, 1)], 10: [("w", 4)], 11: [("y", 10)], 12: [("y", 11)], 13: [("y", 12), ("c", 1, 0, M), ("s", 0, 2)], 14: [("y", 13)], 15: [("y", 14)], 16: [("y", 15)], 17: [("y", 16)], 18: [("y", 17), ("c", 2, 0, M), ("s", 2, 3)], 19: [("y", 18)]}

        def live(s):
            return 0 <= s < NSTEP

        pending = []
        for s in range(NSTEP):
            product(s, 0)
            mine = vector_pieces.get(s, [])
            for i in mine[:1]:
                interleave(i, "v")
            if not mine and live(s - 4):
                quantize_y(s - 4)
            if live(s - 2):
                round_y(s - 2, 0, 2, "v")
            if mine and live(s - 4):
                quantize_y(s - 4)
            for n, i in enumerate(mine):
                if n + 1 < len(mine):
                    interleave(mine[n + 1], "v")
                quantize_blur(i)
            for i in pending:
                quantize_blur(i)
            pending = []
            for i in pool_pieces.get(s, []):
                interleave(i, "g")
                pending.append(i)
            if live(s - 3) and s in scalar_gathers:
                gather_quads(s - 3, True)
            product(s, 1)
            square(s, 0)
            if live(s - 1):
                turn(s - 1, 0)
                turn(s - 1, 1)
            if live(s - 2):
                turn_pairs(s - 2, 0)
                turn_pairs(s - 2, 1)
            for i in scalar_pieces.get(s, []):
                interleave(i, "s")
                pending.insert(0, i)
            if live(s - 3) and s not in scalar_gathers:
                gather_quads(s - 3, False)
            square(s, 1)
            if live(s - 1):
                multiply(s - 1, 0)
                multiply(s - 1, 1)
            for d in dmas.get(s, []):
                if d[0] == "w":
                    dst = out_0[W * d[1] : W * (d[1] + 1), 0:1024]
                    nc.sync.dma_start(out=dst.rearrange("(a p) n -> p a n", p=P), in_=wide[d[1]][:])
                elif d[0] == "y":
                    store_y(d[1], 0, 2)
                elif d[0] == "m":
                    load_meas(*d[1:])
                elif d[0] == "b":
                    load_blur(*d[1:])
                elif d[0] == "c":
                    store_codes(*d[1:])
                else:
                    store_scales(d[1], d[2], nc.sync)

        last = NSTEP - 1
        quantize_y(last - 3)
        round_y(last - 1, 0, 2, "v")
        store_codes(3, 0, 512)
        gather_quads(last - 2, True)
        turn(last, 0)
        turn(last, 1)
        turn_pairs(last - 1, 0)
        turn_pairs(last - 1, 1)
        multiply(last, 0)
        store_y(last, 0, 1)
        round_y(last, 0, 1, "s")
        gather_quads(last - 1, True)
        multiply(last, 1)
        store_y(last, 1, 2)
        quantize_y(last - 2)
        round_y(last, 1, 2, "v")
        quantize_y(last - 1)
        store_codes(3, 512, 1024)
        words = ypairs[last][:].rearrange("m a u p e -> m a u (p e)").bitcast(F32)
        yquads[last] = work.tile([P, 1024], BF16, name="yquads", tag="yquads", bufs=3, align_bytes=64)
        quads = yquads[last][:].bitcast(F32).rearrange("p (a m u) -> p a m u", a=2, u=2)
        for a in range(2):
            bank = psum.tile([P, 2, P], F32, name="acc", tag="acc", bufs=3)
            for u in range(2):
                nc.tensor.transpose(bank[:, u, :], words[:, a, u, :], ident[:])
            if a == 0:
                nc.scalar.copy(out=quads[:, a], in_=bank[:].rearrange("p u m -> p m u"))
            else:
                nc.vector.tensor_copy(out=quads[:, a], in_=bank[:].rearrange("p u m -> p m u"))
        quantize_y(last)
        store_codes(3, 1024, M)
        store_scales(3, 4, nc.scalar)
